import numpy as np
import ml_dtypes


def mxq(x, axis, fmt="e4m3"):
    dtype, down = {"e4m3": (ml_dtypes.float8_e4m3fn, 7), "e5m2": (ml_dtypes.float8_e5m2, 14)}[fmt]
    v = np.moveaxis(np.asarray(x, np.float32).astype(ml_dtypes.bfloat16).astype(np.float64), axis, -1)
    blocks = v.reshape(v.shape[:-1] + (-1, 32))
    amax = np.abs(blocks).max(-1, keepdims=True)
    byte = np.maximum(np.where(amax > 0, np.frexp(amax)[1] - 1 + 127, 0) - down, 1)
    scale = np.exp2(byte - 127.0)
    codes = (blocks / scale).astype(np.float32).astype(dtype).astype(np.float64)
    return np.moveaxis((codes * scale).reshape(v.shape), -1, axis)


WIDE = False


def mx_kscale(k):
    if not WIDE:
        return np.ones(k)
    levels = np.array([10, -10, 5, -5, 0])
    if k % 512:
        return np.exp2(np.random.permutation(np.resize(levels, k // 32))).repeat(32)
    a = np.empty((k // 512, 16))
    for p in range(k // 512):
        a[p, :8] = np.random.permutation(np.resize(levels, 8))
        for g in range(8):
            far = levels[np.abs(levels - a[p, g]) >= 10]
            a[p, g + 8] = far[np.random.randint(len(far))]
    return np.exp2(a.ravel()).repeat(32)


BF16 = ml_dtypes.bfloat16


def bf(x):
    return np.asarray(x, np.float32).astype(BF16)


def f64(x):
    return np.asarray(x).astype(np.float64)


B, S, D, M = 8, 512, 512, 256


def stable_softmax(x, axis):
    ex = np.exp(x - np.max(x, axis=axis, keepdims=True))
    return ex / np.sum(ex, axis=axis, keepdims=True)


def draw0():
    s, r, t = mx_kscale(D), mx_kscale(D), mx_kscale(S)
    h = np.random.standard_normal((B, S, D)) * s
    w1 = np.random.standard_normal((D, M)) / np.sqrt(D) / s[:, None]
    tb = np.random.uniform(-2.5, 0.0, (B, S))
    g = np.random.standard_normal((B, S)) * t
    e = np.random.standard_normal((B, S, D)) * r / t[:, None]
    ws = np.random.standard_normal((D, D)) / np.sqrt(D) / r[:, None]
    c = np.random.standard_normal((B, D))
    return {"h": bf(h), "w1": bf(w1), "tb": bf(tb), "g": bf(g), "e": bf(e), "ws": bf(ws), "c": bf(c)}


def core(h, w1, tb, g, e, ws, c):
    k = mxq(f64(h), 2, "e4m3") @ mxq(f64(w1), 0, "e4m3")
    l = 2.0 * np.tanh(k) + f64(tb)[:, :, None]
    p = stable_softmax(l, 1)
    a = np.sqrt(S) * p * f64(g)[:, :, None]
    u = mxq(f64(e), 2, "e4m3") @ mxq(f64(ws), 0, "e4m3")
    v = mxq(a, 1, "e4m3").transpose(0, 2, 1) @ mxq(u, 1, "e4m3")
    q = np.sum(v * f64(c)[:, None, :], axis=-1) / np.sqrt(D)
    alpha = stable_softmax(q, 1)
    return M * alpha[:, :, None] * v


def e4m3fn_bytes(y):
    return np.clip(np.asarray(y, np.float64), -448.0, 448.0).astype(np.float32).astype(ml_dtypes.float8_e4m3fn).view(np.uint8)


def e4m3fn_values(b):
    return np.asarray(b, np.uint8).view(ml_dtypes.float8_e4m3fn).astype(np.float64)


def setup_inputs():
    d = draw0()
    x0 = np.asarray(d['h']).astype(np.float64)
    s = (np.max(np.abs(x0), axis=(0, 1), keepdims=True) / 448.0).astype(np.float32)
    out = {}
    for k, v in d.items():
        if k == 'h':
            out['h_bytes'] = e4m3fn_bytes(x0 / s.astype(np.float64))
            out['h_scale'] = s
        else:
            out[k] = v
    return out


def reference(h_bytes, h_scale, w1, tb, g, e, ws, c):
    return core(e4m3fn_values(h_bytes) * h_scale.astype(np.float64), w1, tb, g, e, ws, c)

@@ -1,0 +1,371 @@
+import math
+from contextlib import ExitStack
+
+import concourse.mybir as mybir
+from concourse.masks import make_identity
+
+B, S, D, M = 8, 512, 512, 256
+P = 128
+PACK = 4
+FLOPS = 2 * B * S * (D * M + D * D + M * D)
+
+F32 = mybir.dt.float32
+BF16 = mybir.dt.bfloat16
+U32 = mybir.dt.uint32
+U8 = mybir.dt.uint8
+FP8 = mybir.dt.float8_e4m3fn
+FP8X4 = mybir.dt.float8_e4m3fn_x4
+ACT = mybir.ActivationFunctionType
+ALU = mybir.AluOpType
+AXIS = mybir.AxisListType
+
+ORDER = (
+    ("V", 0, 4),
+    ("RC", 0, 3),
+    ("EU", 2, 3),
+    ("U", 3, 3),
+    ("V", 1, 4),
+    ("EU", 3, 3),
+    ("TH", 0, 1),
+    ("TR", 0, 3),
+    ("K", 0, 2),
+    ("K", 1, 2),
+    ("EH", 0, 1),
+    ("TA", 0, 2),
+    ("QV", 0, 4),
+    ("QV", 1, 4),
+    ("U", 1, 3),
+    ("TH", 1, 1),
+    ("AT", 0, 3),
+    ("TA", 1, 2),
+    ("EX", 0, 2),
+    ("EU", 1, 3),
+    ("TQ", 0, 4),
+    ("TE", 0, 1),
+    ("QE", 0, 2),
+    ("MN", 0, 4),
+    ("XE", 0, 4),
+    ("XQ", 0, 4),
+    ("PR", 0, 0),
+    ("RQ", 0, 4),
+    ("U", 2, 2),
+    ("EG", 0, 2),
+    ("U", 0, 2),
+    ("EX", 1, 2),
+    ("TE", 1, 0),
+    ("EH", 1, 1),
+    ("QA", 0, 3),
+    ("AL", 0, 4),
+    ("QU", 0, 3),
+    ("TZ", 0, 2),
+    ("EE", 0, 1),
+    ("O", 0, 4),
+    ("EG", 1, 2),
+    ("O", 1, 4),
+    ("QH", 0, 1),
+    ("EU", 0, 2),
+    ("PR", 1, 0),
+    ("EE", 1, 0),
+)
+
+
+def tile_comireclabelawareinterests_kernel(tc, h_bytes, h_scale, w1, tb, g, e, ws, c, out):
+    nc = tc.nc
+    with ExitStack() as ctx:
+        keep = ctx.enter_context(tc.tile_pool(name="keep", bufs=1))
+        inp = ctx.enter_context(tc.tile_pool(name="inp", bufs=B))
+        work = ctx.enter_context(tc.tile_pool(name="work", bufs=3))
+        psum = ctx.enter_context(tc.psum_pool(name="psum", bufs=1))
+        ctx.enter_context(tc.manual_schedule())
+
+        zero = keep.tile([P, 1], F32)
+        nc.vector.memset(zero[:], 0.0)
+        warm = keep.tile([P, 1], F32)
+        nc.scalar.activation(out=warm[:], in_=zero[:], func=ACT.Exp)
+        rows = keep.tile([P, S], BF16)
+        nc.vector.memset(rows[:], 0.0)
+        ident = keep.tile([P, P], F32)
+        make_identity(nc, ident[:])
+        ident_b = keep.tile([P, P], BF16)
+        make_identity(nc, ident_b[:])
+        ones = keep.tile([P, P], F32)
+        nc.gpsimd.memset(ones[:], 1.0)
+        part = keep.tile([P, P], F32)
+        nc.gpsimd.memset(part[:], 1.0 / M)
+
+        scale2 = keep.tile([P, 2, D], F32)
+        nc.sync.dma_start(out=scale2[:, 0, :], in_=h_scale.rearrange("a b d -> (a b d)").partition_broadcast(P))
+        hbytes, ebf, cb = [], [], []
+        w1_raw = keep.tile([P, PACK, M], BF16)
+        ws_raw = keep.tile([P, PACK, D], BF16)
+        for b in range(B):
+            hb = inp.tile([P, PACK * D], U8)
+            nc.sync.dma_start(out=hb[:], in_=h_bytes[b].rearrange("(p t) d -> p (t d)", t=PACK))
+            hbytes.append(hb)
+            if b == 0:
+                nc.sync.dma_start(out=rows[0:B, :], in_=tb)
+                nc.sync.dma_start(out=rows[B : 2 * B, :], in_=g)
+            eb = inp.tile([P, PACK, D], BF16)
+            nc.sync.dma_start(out=eb[:], in_=e[b].rearrange("(p t) d -> p t d", t=PACK))
+            ebf.append(eb)
+            if b == 0:
+                nc.sync.dma_start(out=w1_raw[:], in_=w1.rearrange("(p j) n -> p j n", j=PACK))
+                nc.sync.dma_start(out=ws_raw[:], in_=ws.rearrange("(p j) n -> p j n", j=PACK))
+            cc = inp.tile([P, D], BF16)
+            nc.sync.dma_start(out=cc[:], in_=c[b : b + 1, :].rearrange("o d -> (o d)").partition_broadcast(P))
+            cb.append(cc)
+        nc.vector.tensor_copy(out=scale2[:, 1, :], in_=scale2[:, 0, :])
+
+        w1_q = keep.tile([P, M], U32, align_bytes=64)
+        w1_s = keep.tile([P, M], U8, align_bytes=64)
+        ws_q = keep.tile([P, D], U32, align_bytes=64)
+        ws_s = keep.tile([P, D], U8, align_bytes=64)
+        bias = keep.tile([P, PACK, B], F32)
+        gain = keep.tile([P, PACK, B], F32)
+
+        def weights():
+            w1_il = keep.tile([P, M, PACK], BF16, align_bytes=64)
+            nc.scalar.copy(out=w1_il[:], in_=w1_raw[:].rearrange("p j n -> p n j"))
+            ws_il = keep.tile([P, D, PACK], BF16, align_bytes=64)
+            nc.vector.tensor_copy(out=ws_il[:], in_=ws_raw[:].rearrange("p j n -> p n j"))
+            nc.vector.quantize_mx(out=w1_q[:].bitcast(FP8X4), scales=w1_s[:], in_=w1_il[:].rearrange("p n j -> p (n j)"))
+            nc.vector.quantize_mx(out=ws_q[:].bitcast(FP8X4), scales=ws_s[:], in_=ws_il[:].rearrange("p n j -> p (n j)"))
+
+        def token_vectors():
+            top = keep.tile([P, 1], F32)
+            nc.vector.tensor_reduce(out=top[:], in_=rows[:], axis=AXIS.X, op=ALU.max)
+            turned = psum.tile([P, PACK, P], BF16, name="turned", tag="small", bufs=1)
+            for t in range(PACK):
+                nc.tensor.transpose(turned[:, t, :], rows[:, t::PACK], ident_b[:])
+            gain_t = gain[:]
+            nc.vector.tensor_scalar(out=gain_t, in0=turned[:, :, B : 2 * B], scalar1=math.sqrt(S), scalar2=None, op0=ALU.mult)
+            tb_t = keep.tile([P, PACK, B], F32)
+            nc.vector.tensor_copy(out=tb_t[:], in_=turned[:, :, 0:B])
+            spread = psum.tile([P, P], F32, name="spread", tag="small", bufs=1)
+            nc.tensor.transpose(spread[:], top[:].to_broadcast([P, P]), ident[:])
+            nc.vector.scalar_tensor_tensor(out=bias[:], in0=tb_t[:], scalar=-2.0, in1=spread[:, 0:B].unsqueeze(1).to_broadcast([P, PACK, B]), op0=ALU.add, op1=ALU.subtract)
+
+        st = [{} for b in range(B)]
+
+        def bank(shape, name):
+            return psum.tile(shape, F32, name=name, tag="bank", bufs=5)
+
+        def widen(b, k):
+            s = st[b]
+            if "hv" not in s:
+                hv = work.tile([P, PACK, D], BF16)
+                s["hv"] = hv
+            nc.vector.tensor_tensor(
+                out=s["hv"][:, 2 * k : 2 * k + 2, :].rearrange("p t d -> p (t d)"),
+                in0=hbytes[b][:, 2 * k * D : (2 * k + 2) * D].bitcast(FP8),
+                in1=scale2[:].rearrange("p t d -> p (t d)"),
+                op=ALU.mult,
+            )
+
+        def turn(b, k, src, key):
+            words = src.rearrange("p t d -> p (t d)").bitcast(F32).rearrange("p (t w) -> p t w", t=PACK)
+            pt = bank([P, 2, 2, P], key)
+            for i in range(2):
+                for u in range(2):
+                    nc.tensor.transpose(pt[:, i, u, :], words[:, 2 * k + i, u :: 2], ident[:])
+            st[b][key + str(k)] = pt
+
+        def lay(b, k, key, eng):
+            s = st[b]
+            if key + "_il" not in s:
+                il = work.tile([P, S * PACK], BF16, name=key + "_il", align_bytes=64)
+                s[key + "_il"] = il
+            o = s[key + "_il"][:].bitcast(F32)[:, 512 * k : 512 * k + 512].rearrange("p (i r u) -> p i r u", i=2, u=2)
+            i_ = s[key + str(k)][:].rearrange("p i u r -> p i r u")
+            copy(eng, o, i_)
+
+        def copy(eng, o, i_):
+            if eng == "S":
+                nc.scalar.copy(out=o, in_=i_)
+            else:
+                nc.vector.tensor_copy(out=o, in_=i_)
+
+        def quant(b, key, width):
+            q = work.tile([P, width], U32, name=key + "_q", align_bytes=64)
+            sc = work.tile([P, width], U8, name=key + "_s", align_bytes=64)
+            nc.vector.quantize_mx(out=q[:].bitcast(FP8X4), scales=sc[:], in_=st[b][key + "_il"][:])
+            st[b][key + "_q"] = q
+            st[b][key + "_s"] = sc
+
+        def mx(o, lq, ls, lc, rq, rs, rc):
+            nc.tensor.matmul_mx(out=o, lhsT=lq[:, lc].bitcast(FP8X4), lhsT_scale=ls[:, lc], rhs=rq[:, rc].bitcast(FP8X4), rhs_scale=rs[:, rc], start=True, stop=True)
+
+        def score(b, k):
+            pk = bank([P, 2, M], "pk")
+            s = st[b]
+            for i in range(2):
+                t = 2 * k + i
+                mx(pk[:, i, :], s["h_q"], s["h_s"], slice(t * P, (t + 1) * P), w1_q, w1_s, slice(0, M))
+            s["pk" + str(k)] = pk
+
+        def tanh(b, k):
+            s = st[b]
+            if "th" not in s:
+                th = work.tile([P, PACK, M], F32)
+                s["th"] = th
+            nc.scalar.activation(out=s["th"][:, 2 * k : 2 * k + 2, :], in_=s["pk" + str(k)][:], func=ACT.Tanh)
+
+        def expo(b, k):
+            s = st[b]
+            if "ex" not in s:
+                ex = work.tile([P, PACK, M], F32)
+                s["ex"] = ex
+            for t in (2 * k, 2 * k + 1):
+                nc.scalar.activation(out=s["ex"][:, t, :], in_=s["th"][:, t, :], func=ACT.Exp, bias=bias[:, t, b : b + 1], scale=2.0)
+
+        def gained(b, k):
+            s = st[b]
+            if "eg" not in s:
+                eg = work.tile([P, PACK, M], F32)
+                s["eg"] = eg
+            for t in (2 * k, 2 * k + 1):
+                nc.vector.tensor_scalar(out=s["eg"][:, t, :], in0=s["ex"][:, t, :], scalar1=gain[:, t, b : b + 1], scalar2=None, op0=ALU.mult)
+
+        def total(b):
+            s = st[b]
+            pz = psum.tile([P, 512], F32, name="pz", tag="small", bufs=1)
+            s["pz"] = pz
+            for j in range(2):
+                for t in range(PACK):
+                    nc.tensor.matmul(pz[:, 64 * j : 64 * j + 64], lhsT=s["ex"][:, t, j * P : (j + 1) * P], rhs=ones[:, 0:64], start=(t == 0), stop=(t == PACK - 1))
+
+        def recip(b):
+            s = st[b]
+            rz = work.tile([P, 2], F32)
+            nc.vector.reciprocal(out=rz[:], in_=s["pz"][:, 0:128:64])
+            s["rz"] = rz
+
+        def spread_total(b):
+            s = st[b]
+            for j in range(2):
+                nc.tensor.transpose(s["pz"][:, M + j * P : M + (j + 1) * P], s["rz"][:, j : j + 1].to_broadcast([P, P]), ident[:])
+
+        def weight(b):
+            s = st[b]
+            a_il = work.tile([P, M * PACK], BF16, align_bytes=64)
+            s["a_il"] = a_il
+            nc.vector.tensor_tensor(
+                out=a_il[:].rearrange("p (m t) -> p m t", t=PACK),
+                in0=s["eg"][:].rearrange("p t m -> p m t"),
+                in1=s["pz"][:, M : 2 * M].unsqueeze(2).to_broadcast([P, M, PACK]),
+                op=ALU.mult,
+            )
+
+        def project(b, n):
+            s = st[b]
+            pu = bank([P, PACK, P], "pu")
+            for t in range(PACK):
+                mx(pu[:, t, :], s["e_q"], s["e_s"], slice(t * P, (t + 1) * P), ws_q, ws_s, slice(n * P, (n + 1) * P))
+            s["pu" + str(n)] = pu
+
+        def lay_u(b, n, eng):
+            s = st[b]
+            if "u_il" not in s:
+                u_il = work.tile([P, D * PACK], BF16, align_bytes=64)
+                s["u_il"] = u_il
+            copy(eng, s["u_il"][:, 512 * n : 512 * n + 512].rearrange("p (n t) -> p n t", t=PACK), s["pu" + str(n)][:].rearrange("p t n -> p n t"))
+
+        def pool_v(b, j):
+            s = st[b]
+            pv = psum.tile([P, D], F32, name="pv", tag="pv", bufs=2)
+            mx(pv[:], s["a_q"], s["a_s"], slice(j * P, (j + 1) * P), s["u_q"], s["u_s"], slice(0, D))
+            s["pv" + str(j)] = pv
+
+        def logit(b, j):
+            s = st[b]
+            if "nq" not in s:
+                nq = work.tile([P, 2], F32)
+                s["nq"] = nq
+            junk = work.tile([P, D], F32)
+            nc.vector.scalar_tensor_tensor(out=junk[:], in0=s["pv" + str(j)][:], scalar=-1.0 / math.sqrt(D), in1=cb[b][:], op0=ALU.mult, op1=ALU.mult, accum_out=s["nq"][:, j : j + 1])
+
+        def spread_logit(b):
+            s = st[b]
+            pq = psum.tile([P, 512], F32, name="pq", tag="small", bufs=1)
+            s["pq"] = pq
+            for j in range(2):
+                nc.tensor.transpose(pq[:, j * P : (j + 1) * P], s["nq"][:, j : j + 1].to_broadcast([P, P]), ident[:])
+
+        def least(b):
+            s = st[b]
+            mn = work.tile([P, 1], F32)
+            nc.vector.tensor_reduce(out=mn[:], in_=s["pq"][:, 0:M], axis=AXIS.X, op=ALU.min)
+            s["mn"] = mn
+
+        def exp_q(b):
+            s = st[b]
+            xq = work.tile([P, 2], F32)
+            nc.scalar.activation(out=xq[:], in_=s["nq"][:], func=ACT.Exp, bias=s["mn"][:], scale=-1.0)
+            s["xq"] = xq
+
+        def sum_q(b):
+            s = st[b]
+            for j in range(2):
+                nc.tensor.matmul(s["pq"][:, M : M + 1], lhsT=part[:], rhs=s["xq"][:, j : j + 1], start=(j == 0), stop=(j == 1))
+
+        def recip_q(b):
+            s = st[b]
+            rq = work.tile([P, 1], F32)
+            nc.vector.reciprocal(out=rq[:], in_=s["pq"][:, M : M + 1])
+            s["rq"] = rq
+
+        def alpha(b):
+            s = st[b]
+            al = work.tile([P, 2], F32)
+            nc.scalar.activation(out=al[:], in_=s["xq"][:], func=ACT.Copy, scale=s["rq"][:])
+            s["al"] = al
+
+        def finish(b, j):
+            s = st[b]
+            o = work.tile([P, D], F32, name="o", bufs=4)
+            nc.scalar.activation(out=o[:], in_=s["pv" + str(j)][:], func=ACT.Copy, scale=s["al"][:, j : j + 1])
+            nc.sync.dma_start(out=out[b, j * P : (j + 1) * P, :], in_=o[:])
+
+        steps = {
+            "PR": widen,
+            "TH": lambda b, k: turn(b, k, st[b]["hv"][:], "h"),
+            "TE": lambda b, k: turn(b, k, ebf[b][:], "e"),
+            "EH": lambda b, k: lay(b, k, "h", "S"),
+            "EE": lambda b, k: lay(b, k, "e", "S"),
+            "QH": lambda b, k: quant(b, "h", S),
+            "QE": lambda b, k: quant(b, "e", S),
+            "K": score,
+            "TA": tanh,
+            "EX": expo,
+            "EG": gained,
+            "TZ": lambda b, k: total(b),
+            "RC": lambda b, k: recip(b),
+            "TR": lambda b, k: spread_total(b),
+            "AT": lambda b, k: weight(b),
+            "QA": lambda b, k: quant(b, "a", M),
+            "U": project,
+            "EU": lambda b, k: lay_u(b, k, "S"),
+            "QU": lambda b, k: quant(b, "u", D),
+            "V": pool_v,
+            "QV": logit,
+            "TQ": lambda b, k: spread_logit(b),
+            "MN": lambda b, k: least(b),
+            "XE": lambda b, k: exp_q(b),
+            "XQ": lambda b, k: sum_q(b),
+            "RQ": lambda b, k: recip_q(b),
+            "AL": lambda b, k: alpha(b),
+            "O": finish,
+        }
+        last = max(lag for name, k, lag in ORDER)
+        ready = set()
+        for i in range(B + last):
+            for name, k, lag in ORDER:
+                b = i - lag
+                if 0 <= b < B:
+                    if name in ("K", "U") and "w" not in ready:
+                        ready.add("w")
+                        weights()
+                    if name == "EX" and "t" not in ready:
+                        ready.add("t")
+                        token_vectors()
+                    steps[name](b, k)

@@ -21,51 +21,53 @@ AXIS = mybir.AxisListType
 
 ORDER = (
     ("V", 0, 4),
+    ("U", 1, 3),
     ("RC", 0, 3),
-    ("EU", 2, 3),
-    ("U", 3, 3),
     ("V", 1, 4),
+    ("U", 3, 3),
     ("EU", 3, 3),
+    ("EU", 1, 3),
+    ("QV", 0, 4),
     ("TH", 0, 1),
     ("TR", 0, 3),
-    ("K", 0, 2),
-    ("K", 1, 2),
     ("EH", 0, 1),
-    ("TA", 0, 2),
-    ("QV", 0, 4),
+    ("K", 0, 2),
     ("QV", 1, 4),
-    ("U", 1, 3),
-    ("TH", 1, 1),
     ("AT", 0, 3),
+    ("K", 1, 2),
+    ("TH", 1, 1),
+    ("QE", 0, 2),
+    ("TA", 0, 2),
     ("TA", 1, 2),
-    ("EX", 0, 2),
-    ("EU", 1, 3),
+    ("QA", 0, 3),
     ("TQ", 0, 4),
     ("TE", 0, 1),
-    ("QE", 0, 2),
     ("MN", 0, 4),
-    ("XE", 0, 4),
-    ("XQ", 0, 4),
     ("PR", 0, 0),
+    ("EX", 0, 2),
+    ("XE", 0, 4),
+    ("TE", 1, 0),
+    ("XQ", 0, 4),
+    ("XS", 0, 4),
+    ("EX", 1, 2),
+    ("EG", 0, 2),
     ("RQ", 0, 4),
     ("U", 2, 2),
-    ("EG", 0, 2),
-    ("U", 0, 2),
-    ("EX", 1, 2),
-    ("TE", 1, 0),
-    ("EH", 1, 1),
-    ("QA", 0, 3),
-    ("AL", 0, 4),
     ("QU", 0, 3),
     ("TZ", 0, 2),
+    ("EH", 1, 1),
     ("EE", 0, 1),
-    ("O", 0, 4),
     ("EG", 1, 2),
-    ("O", 1, 4),
     ("QH", 0, 1),
-    ("EU", 0, 2),
-    ("PR", 1, 0),
+    ("AL", 0, 4),
+    ("O", 0, 4),
+    ("ZR", 0, 2),
+    ("U", 0, 2),
+    ("O", 1, 4),
+    ("EU", 2, 2),
     ("EE", 1, 0),
+    ("PR", 1, 0),
+    ("EU", 0, 2),
 )
 
 
@@ -88,10 +90,6 @@ def tile_comireclabelawareinterests_kernel(tc, h_bytes, h_scale, w1, tb, g, e, w
         make_identity(nc, ident[:])
         ident_b = keep.tile([P, P], BF16)
         make_identity(nc, ident_b[:])
-        ones = keep.tile([P, P], F32)
-        nc.gpsimd.memset(ones[:], 1.0)
-        part = keep.tile([P, P], F32)
-        nc.gpsimd.memset(part[:], 1.0 / M)
 
         scale2 = keep.tile([P, 2, D], F32)
         nc.sync.dma_start(out=scale2[:, 0, :], in_=h_scale.rearrange("a b d -> (a b d)").partition_broadcast(P))
@@ -232,12 +230,18 @@ def tile_comireclabelawareinterests_kernel(tc, h_bytes, h_scale, w1, tb, g, e, w
             s["pz"] = pz
             for j in range(2):
                 for t in range(PACK):
-                    nc.tensor.matmul(pz[:, 64 * j : 64 * j + 64], lhsT=s["ex"][:, t, j * P : (j + 1) * P], rhs=ones[:, 0:64], start=(t == 0), stop=(t == PACK - 1))
+                    nc.tensor.matmul(pz[:, j * P : (j + 1) * P], lhsT=s["ex"][:, t, j * P : (j + 1) * P], rhs=ident[:], is_transpose=True, start=(t == 0), stop=(t == PACK - 1))
+
+        def sum_z(b):
+            s = st[b]
+            zz = work.tile([P, 2], F32)
+            nc.vector.tensor_reduce(out=zz[:], in_=s["pz"][:, 0:M].rearrange("p (j r) -> p j r", j=2), axis=AXIS.X, op=ALU.add)
+            s["zz"] = zz
 
         def recip(b):
             s = st[b]
             rz = work.tile([P, 2], F32)
-            nc.vector.reciprocal(out=rz[:], in_=s["pz"][:, 0:128:64])
+            nc.vector.reciprocal(out=rz[:], in_=s["zz"][:])
             s["rz"] = rz
 
         def spread_total(b):
@@ -306,18 +310,24 @@ def tile_comireclabelawareinterests_kernel(tc, h_bytes, h_scale, w1, tb, g, e, w
         def sum_q(b):
             s = st[b]
             for j in range(2):
-                nc.tensor.matmul(s["pq"][:, M : M + 1], lhsT=part[:], rhs=s["xq"][:, j : j + 1], start=(j == 0), stop=(j == 1))
+                nc.tensor.matmul(s["pq"][:, M : M + P], lhsT=s["xq"][:, j : j + 1].to_broadcast([P, P]), rhs=ident[:], is_transpose=True, start=(j == 0), stop=(j == 1))
+
+        def add_q(b):
+            s = st[b]
+            sq = work.tile([P, 1], F32)
+            nc.vector.tensor_reduce(out=sq[:], in_=s["pq"][:, M : M + P], axis=AXIS.X, op=ALU.add)
+            s["sq"] = sq
 
         def recip_q(b):
             s = st[b]
             rq = work.tile([P, 1], F32)
-            nc.vector.reciprocal(out=rq[:], in_=s["pq"][:, M : M + 1])
+            nc.vector.reciprocal(out=rq[:], in_=s["sq"][:])
             s["rq"] = rq
 
         def alpha(b):
             s = st[b]
             al = work.tile([P, 2], F32)
-            nc.scalar.activation(out=al[:], in_=s["xq"][:], func=ACT.Copy, scale=s["rq"][:])
+            nc.vector.tensor_scalar(out=al[:], in0=s["xq"][:], scalar1=s["rq"][:], scalar2=float(M), op0=ALU.mult, op1=ALU.mult)
             s["al"] = al
 
         def finish(b, j):
@@ -339,6 +349,8 @@ def tile_comireclabelawareinterests_kernel(tc, h_bytes, h_scale, w1, tb, g, e, w
             "EX": expo,
             "EG": gained,
             "TZ": lambda b, k: total(b),
+            "ZR": lambda b, k: sum_z(b),
+            "XS": lambda b, k: add_q(b),
             "RC": lambda b, k: recip(b),
             "TR": lambda b, k: spread_total(b),
             "AT": lambda b, k: weight(b),

@@ -20,54 +20,53 @@ ALU = mybir.AluOpType
 AXIS = mybir.AxisListType
 
 ORDER = (
-    ("V", 0, 4),
+    ("QV", 0, 5),
+    ("K", 1, 3),
+    ("TA", 1, 3),
+    ("EG", 0, 4),
+    ("TR", 0, 4),
+    ("TE", 0, 1),
+    ("PR", 1, 1),
+    ("TQ", 0, 5),
+    ("EE", 0, 1),
+    ("EX", 0, 3),
+    ("MN", 0, 5),
+    ("XQ", 0, 5),
+    ("U", 2, 3),
+    ("XE", 0, 5),
+    ("AT", 0, 4),
+    ("TH", 0, 1),
+    ("TH", 1, 1),
+    ("EX", 1, 3),
+    ("TE", 1, 0),
+    ("RQ", 0, 5),
+    ("QH", 0, 2),
+    ("TZ", 0, 3),
+    ("EU", 2, 3),
+    ("AL", 0, 5),
+    ("K", 0, 2),
+    ("QU", 0, 4),
+    ("EH", 0, 1),
+    ("QA", 0, 4),
+    ("EG", 1, 3),
     ("U", 1, 3),
-    ("RC", 0, 3),
+    ("PR", 0, 0),
+    ("O", 1, 5),
+    ("O", 0, 5),
+    ("EH", 1, 1),
     ("V", 1, 4),
+    ("V", 0, 4),
+    ("ZR", 0, 3),
+    ("EE", 1, 0),
+    ("QE", 0, 2),
+    ("U", 0, 3),
+    ("RC", 0, 3),
+    ("QV", 1, 4),
+    ("TA", 0, 2),
+    ("EU", 1, 3),
+    ("EU", 0, 3),
     ("U", 3, 3),
     ("EU", 3, 3),
-    ("EU", 1, 3),
-    ("QV", 0, 4),
-    ("TH", 0, 1),
-    ("TR", 0, 3),
-    ("EH", 0, 1),
-    ("K", 0, 2),
-    ("QV", 1, 4),
-    ("AT", 0, 3),
-    ("K", 1, 2),
-    ("TH", 1, 1),
-    ("QE", 0, 2),
-    ("TA", 0, 2),
-    ("TA", 1, 2),
-    ("QA", 0, 3),
-    ("TQ", 0, 4),
-    ("TE", 0, 1),
-    ("MN", 0, 4),
-    ("PR", 0, 0),
-    ("EX", 0, 2),
-    ("XE", 0, 4),
-    ("TE", 1, 0),
-    ("XQ", 0, 4),
-    ("XS", 0, 4),
-    ("EX", 1, 2),
-    ("EG", 0, 2),
-    ("RQ", 0, 4),
-    ("U", 2, 2),
-    ("QU", 0, 3),
-    ("TZ", 0, 2),
-    ("EH", 1, 1),
-    ("EE", 0, 1),
-    ("EG", 1, 2),
-    ("QH", 0, 1),
-    ("AL", 0, 4),
-    ("O", 0, 4),
-    ("ZR", 0, 2),
-    ("U", 0, 2),
-    ("O", 1, 4),
-    ("EU", 2, 2),
-    ("EE", 1, 0),
-    ("PR", 1, 0),
-    ("EU", 0, 2),
 )
 
 
@@ -92,8 +91,10 @@ def tile_comireclabelawareinterests_kernel(tc, h_bytes, h_scale, w1, tb, g, e, w
         make_identity(nc, ident_b[:])
 
         scale2 = keep.tile([P, 2, D], F32)
-        nc.sync.dma_start(out=scale2[:, 0, :], in_=h_scale.rearrange("a b d -> (a b d)").partition_broadcast(P))
-        hbytes, ebf, cb = [], [], []
+        scale_col = keep.tile([P, D // P], F32)
+        with nc.allow_non_contiguous_dma(reason="512 scales, one pass"):
+            nc.sync.dma_start(out=scale_col[:], in_=h_scale.rearrange("a b (k p) -> p (a b k)", p=P))
+        hbytes, ebf = [], []
         w1_raw = keep.tile([P, PACK, M], BF16)
         ws_raw = keep.tile([P, PACK, D], BF16)
         for b in range(B):
@@ -109,10 +110,14 @@ def tile_comireclabelawareinterests_kernel(tc, h_bytes, h_scale, w1, tb, g, e, w
             if b == 0:
                 nc.sync.dma_start(out=w1_raw[:], in_=w1.rearrange("(p j) n -> p j n", j=PACK))
                 nc.sync.dma_start(out=ws_raw[:], in_=ws.rearrange("(p j) n -> p j n", j=PACK))
-            cc = inp.tile([P, D], BF16)
-            nc.sync.dma_start(out=cc[:], in_=c[b : b + 1, :].rearrange("o d -> (o d)").partition_broadcast(P))
-            cb.append(cc)
-        nc.vector.tensor_copy(out=scale2[:, 1, :], in_=scale2[:, 0, :])
+            if b == 1:
+                c_all = keep.tile([P, B, D], BF16)
+                nc.sync.dma_start(out=c_all[:].rearrange("p b d -> p (b d)"), in_=c.rearrange("b d -> (b d)").partition_broadcast(P))
+        scale_ps = psum.tile([P, D], F32, name="scale_ps", tag="small", bufs=2)
+        for k in range(D // P):
+            nc.tensor.transpose(scale_ps[:, k * P : (k + 1) * P], scale_col[:, k : k + 1].to_broadcast([P, P]), ident[:])
+        nc.vector.tensor_copy(out=scale2[:, 0, :], in_=scale_ps[:])
+        nc.scalar.copy(out=scale2[:, 1, :], in_=scale_ps[:])
 
         w1_q = keep.tile([P, M], U32, align_bytes=64)
         w1_s = keep.tile([P, M], U8, align_bytes=64)
@@ -132,21 +137,21 @@ def tile_comireclabelawareinterests_kernel(tc, h_bytes, h_scale, w1, tb, g, e, w
         def token_vectors():
             top = keep.tile([P, 1], F32)
             nc.vector.tensor_reduce(out=top[:], in_=rows[:], axis=AXIS.X, op=ALU.max)
-            turned = psum.tile([P, PACK, P], BF16, name="turned", tag="small", bufs=1)
+            turned = psum.tile([P, PACK, P], BF16, name="turned", tag="small", bufs=2)
             for t in range(PACK):
                 nc.tensor.transpose(turned[:, t, :], rows[:, t::PACK], ident_b[:])
             gain_t = gain[:]
             nc.vector.tensor_scalar(out=gain_t, in0=turned[:, :, B : 2 * B], scalar1=math.sqrt(S), scalar2=None, op0=ALU.mult)
             tb_t = keep.tile([P, PACK, B], F32)
             nc.vector.tensor_copy(out=tb_t[:], in_=turned[:, :, 0:B])
-            spread = psum.tile([P, P], F32, name="spread", tag="small", bufs=1)
+            spread = psum.tile([P, P], F32, name="spread", tag="small", bufs=2)
             nc.tensor.transpose(spread[:], top[:].to_broadcast([P, P]), ident[:])
             nc.vector.scalar_tensor_tensor(out=bias[:], in0=tb_t[:], scalar=-2.0, in1=spread[:, 0:B].unsqueeze(1).to_broadcast([P, PACK, B]), op0=ALU.add, op1=ALU.subtract)
 
         st = [{} for b in range(B)]
 
         def bank(shape, name):
-            return psum.tile(shape, F32, name=name, tag="bank", bufs=5)
+            return psum.tile(shape, F32, name=name, tag="bank", bufs=4)
 
         def widen(b, k):
             s = st[b]
@@ -226,7 +231,7 @@ def tile_comireclabelawareinterests_kernel(tc, h_bytes, h_scale, w1, tb, g, e, w
 
         def total(b):
             s = st[b]
-            pz = psum.tile([P, 512], F32, name="pz", tag="small", bufs=1)
+            pz = psum.tile([P, 512], F32, name="pz", tag="small", bufs=2)
             s["pz"] = pz
             for j in range(2):
                 for t in range(PACK):
@@ -254,9 +259,9 @@ def tile_comireclabelawareinterests_kernel(tc, h_bytes, h_scale, w1, tb, g, e, w
             a_il = work.tile([P, M * PACK], BF16, align_bytes=64)
             s["a_il"] = a_il
             nc.vector.tensor_tensor(
-                out=a_il[:].rearrange("p (m t) -> p m t", t=PACK),
-                in0=s["eg"][:].rearrange("p t m -> p m t"),
-                in1=s["pz"][:, M : 2 * M].unsqueeze(2).to_broadcast([P, M, PACK]),
+                out=a_il[:].rearrange("p (m i t) -> p m t i", i=PACK, t=PACK),
+                in0=s["eg"][:].rearrange("p t (m i) -> p m t i", i=PACK),
+                in1=s["pz"][:, M : 2 * M].rearrange("p (m i) -> p m i", i=PACK).unsqueeze(2).to_broadcast([P, M // PACK, PACK, PACK]),
                 op=ALU.mult,
             )
 
@@ -286,11 +291,11 @@ def tile_comireclabelawareinterests_kernel(tc, h_bytes, h_scale, w1, tb, g, e, w
                 nq = work.tile([P, 2], F32)
                 s["nq"] = nq
             junk = work.tile([P, D], F32)
-            nc.vector.scalar_tensor_tensor(out=junk[:], in0=s["pv" + str(j)][:], scalar=-1.0 / math.sqrt(D), in1=cb[b][:], op0=ALU.mult, op1=ALU.mult, accum_out=s["nq"][:, j : j + 1])
+            nc.vector.scalar_tensor_tensor(out=junk[:], in0=s["pv" + str(j)][:], scalar=-1.0 / math.sqrt(D), in1=c_all[:, b, :], op0=ALU.mult, op1=ALU.mult, accum_out=s["nq"][:, j : j + 1])
 
         def spread_logit(b):
             s = st[b]
-            pq = psum.tile([P, 512], F32, name="pq", tag="small", bufs=1)
+            pq = psum.tile([P, 512], F32, name="pq", tag="small", bufs=2)
             s["pq"] = pq
             for j in range(2):
                 nc.tensor.transpose(pq[:, j * P : (j + 1) * P], s["nq"][:, j : j + 1].to_broadcast([P, P]), ident[:])
@@ -309,19 +314,15 @@ def tile_comireclabelawareinterests_kernel(tc, h_bytes, h_scale, w1, tb, g, e, w
 
         def sum_q(b):
             s = st[b]
-            for j in range(2):
-                nc.tensor.matmul(s["pq"][:, M : M + P], lhsT=s["xq"][:, j : j + 1].to_broadcast([P, P]), rhs=ident[:], is_transpose=True, start=(j == 0), stop=(j == 1))
-
-        def add_q(b):
-            s = st[b]
-            sq = work.tile([P, 1], F32)
-            nc.vector.tensor_reduce(out=sq[:], in_=s["pq"][:, M : M + P], axis=AXIS.X, op=ALU.add)
-            s["sq"] = sq
+            zq = work.tile([P, 1], F32)
+            junk_q = work.tile([P, M], F32)
+            nc.scalar.activation(out=junk_q[:], in_=s["pq"][:, 0:M], func=ACT.Exp, bias=s["mn"][:], scale=-1.0, accum_out=zq[:])
+            s["zq"] = zq
 
         def recip_q(b):
             s = st[b]
             rq = work.tile([P, 1], F32)
-            nc.vector.reciprocal(out=rq[:], in_=s["sq"][:])
+            nc.vector.reciprocal(out=rq[:], in_=s["zq"][:])
             s["rq"] = rq
 
         def alpha(b):
@@ -350,7 +351,6 @@ def tile_comireclabelawareinterests_kernel(tc, h_bytes, h_scale, w1, tb, g, e, w
             "EG": gained,
             "TZ": lambda b, k: total(b),
             "ZR": lambda b, k: sum_z(b),
-            "XS": lambda b, k: add_q(b),
             "RC": lambda b, k: recip(b),
             "TR": lambda b, k: spread_total(b),
             "AT": lambda b, k: weight(b),

@@ -20,53 +20,53 @@ ALU = mybir.AluOpType
 AXIS = mybir.AxisListType
 
 ORDER = (
-    ("QV", 0, 5),
-    ("K", 1, 3),
-    ("TA", 1, 3),
-    ("EG", 0, 4),
-    ("TR", 0, 4),
-    ("TE", 0, 1),
+    ("EH", 1, 3),
+    ("ZR", 0, 5),
+    ("EG", 0, 5),
+    ("EG", 1, 5),
+    ("TA", 0, 4),
+    ("EU", 2, 5),
+    ("V", 0, 6),
+    ("TA", 1, 4),
+    ("RC", 0, 5),
+    ("U", 1, 5),
+    ("EX", 0, 4),
+    ("QV", 1, 6),
+    ("QV", 0, 6),
+    ("U", 0, 5),
+    ("EU", 1, 5),
+    ("QH", 0, 3),
     ("PR", 1, 1),
-    ("TQ", 0, 5),
-    ("EE", 0, 1),
-    ("EX", 0, 3),
-    ("MN", 0, 5),
-    ("XQ", 0, 5),
-    ("U", 2, 3),
-    ("XE", 0, 5),
-    ("AT", 0, 4),
-    ("TH", 0, 1),
-    ("TH", 1, 1),
-    ("EX", 1, 3),
-    ("TE", 1, 0),
-    ("RQ", 0, 5),
-    ("QH", 0, 2),
-    ("TZ", 0, 3),
-    ("EU", 2, 3),
-    ("AL", 0, 5),
-    ("K", 0, 2),
-    ("QU", 0, 4),
-    ("EH", 0, 1),
-    ("QA", 0, 4),
-    ("EG", 1, 3),
-    ("U", 1, 3),
+    ("U", 3, 5),
+    ("TR", 0, 5),
+    ("TQ", 0, 6),
+    ("EU", 0, 5),
+    ("EU", 3, 5),
+    ("MN", 0, 6),
+    ("TE", 1, 3),
+    ("EX", 1, 4),
+    ("TH", 0, 2),
+    ("XQ", 0, 6),
+    ("XE", 0, 6),
+    ("AT", 0, 5),
+    ("EE", 1, 3),
+    ("TE", 0, 3),
+    ("RQ", 0, 6),
+    ("EH", 0, 2),
+    ("TH", 1, 2),
+    ("TZ", 0, 4),
+    ("QE", 0, 4),
+    ("AL", 0, 6),
+    ("QA", 0, 5),
+    ("K", 0, 3),
+    ("QU", 0, 5),
+    ("EE", 0, 3),
+    ("U", 2, 4),
+    ("O", 1, 6),
     ("PR", 0, 0),
-    ("O", 1, 5),
-    ("O", 0, 5),
-    ("EH", 1, 1),
-    ("V", 1, 4),
-    ("V", 0, 4),
-    ("ZR", 0, 3),
-    ("EE", 1, 0),
-    ("QE", 0, 2),
-    ("U", 0, 3),
-    ("RC", 0, 3),
-    ("QV", 1, 4),
-    ("TA", 0, 2),
-    ("EU", 1, 3),
-    ("EU", 0, 3),
-    ("U", 3, 3),
-    ("EU", 3, 3),
+    ("O", 0, 6),
+    ("V", 1, 5),
+    ("K", 1, 3),
 )
 
 
@@ -81,43 +81,63 @@ def tile_comireclabelawareinterests_kernel(tc, h_bytes, h_scale, w1, tb, g, e, w
 
         zero = keep.tile([P, 1], F32)
         nc.vector.memset(zero[:], 0.0)
-        warm = keep.tile([P, 1], F32)
-        nc.scalar.activation(out=warm[:], in_=zero[:], func=ACT.Exp)
+        scale_rows = keep.tile([P, P], F32)
+        nc.vector.memset(scale_rows[:], 0.0)
         rows = keep.tile([P, S], BF16)
         nc.vector.memset(rows[:], 0.0)
+        nc.sync.dma_start(out=scale_rows[0 : D // P, :], in_=h_scale.rearrange("a b (k p) -> (a b k) p", p=P))
+        nc.sync.dma_start(out=rows[0:B, :], in_=tb)
+        nc.sync.dma_start(out=rows[B : 2 * B, :], in_=g)
+        warm = keep.tile([P, 1], F32)
+        nc.scalar.activation(out=warm[:], in_=zero[:], func=ACT.Exp)
         ident = keep.tile([P, P], F32)
         make_identity(nc, ident[:])
         ident_b = keep.tile([P, P], BF16)
         make_identity(nc, ident_b[:])
 
-        scale2 = keep.tile([P, 2, D], F32)
-        scale_col = keep.tile([P, D // P], F32)
-        with nc.allow_non_contiguous_dma(reason="512 scales, one pass"):
-            nc.sync.dma_start(out=scale_col[:], in_=h_scale.rearrange("a b (k p) -> p (a b k)", p=P))
-        hbytes, ebf = [], []
         w1_raw = keep.tile([P, PACK, M], BF16)
         ws_raw = keep.tile([P, PACK, D], BF16)
+        nc.sync.dma_start(out=w1_raw[:], in_=w1.rearrange("(p j) n -> p j n", j=PACK))
+        hbytes, ebf = [], []
         for b in range(B):
             hb = inp.tile([P, PACK * D], U8)
             nc.sync.dma_start(out=hb[:], in_=h_bytes[b].rearrange("(p t) d -> p (t d)", t=PACK))
             hbytes.append(hb)
-            if b == 0:
-                nc.sync.dma_start(out=rows[0:B, :], in_=tb)
-                nc.sync.dma_start(out=rows[B : 2 * B, :], in_=g)
             eb = inp.tile([P, PACK, D], BF16)
-            nc.sync.dma_start(out=eb[:], in_=e[b].rearrange("(p t) d -> p t d", t=PACK))
-            ebf.append(eb)
+            e_rows = e[b].rearrange("(p t) d -> p t d", t=PACK)
             if b == 0:
-                nc.sync.dma_start(out=w1_raw[:], in_=w1.rearrange("(p j) n -> p j n", j=PACK))
+                nc.sync.dma_start(out=eb[:, 0:2, :], in_=e_rows[:, 0:2, :])
+                nc.sync.dma_start(out=eb[:, 2:4, :], in_=e_rows[:, 2:4, :])
                 nc.sync.dma_start(out=ws_raw[:], in_=ws.rearrange("(p j) n -> p j n", j=PACK))
+            else:
+                nc.sync.dma_start(out=eb[:], in_=e_rows)
+            ebf.append(eb)
             if b == 1:
                 c_all = keep.tile([P, B, D], BF16)
                 nc.sync.dma_start(out=c_all[:].rearrange("p b d -> p (b d)"), in_=c.rearrange("b d -> (b d)").partition_broadcast(P))
-        scale_ps = psum.tile([P, D], F32, name="scale_ps", tag="small", bufs=2)
-        for k in range(D // P):
-            nc.tensor.transpose(scale_ps[:, k * P : (k + 1) * P], scale_col[:, k : k + 1].to_broadcast([P, P]), ident[:])
-        nc.vector.tensor_copy(out=scale2[:, 0, :], in_=scale_ps[:])
-        nc.scalar.copy(out=scale2[:, 1, :], in_=scale_ps[:])
+
+        scale_turned = psum.tile([P, P], F32, name="scale_turned", tag="small", bufs=2)
+        nc.tensor.transpose(scale_turned[:], scale_rows[:], ident[:])
+        scale_col = keep.tile([P, D // P], F32)
+        nc.vector.tensor_copy(out=scale_col[:], in_=scale_turned[:, 0 : D // P])
+        top = keep.tile([P, 1], F32)
+        nc.vector.tensor_reduce(out=top[:], in_=rows[:], axis=AXIS.X, op=ALU.max)
+        w1_il = keep.tile([P, M, PACK], BF16, align_bytes=64)
+        nc.vector.tensor_copy(out=w1_il[:], in_=w1_raw[:].rearrange("p j n -> p n j"))
+        scale2 = keep.tile([P, 2, D], F32)
+        for i in range(2):
+            scale_ps = psum.tile([P, D], F32, name="scale_ps", tag="bank", bufs=4)
+            for k in range(D // P):
+                nc.tensor.transpose(scale_ps[:, k * P : (k + 1) * P], scale_col[:, k : k + 1].to_broadcast([P, P]), ident[:])
+            if i == 0:
+                nc.vector.tensor_copy(out=scale2[:, 0, :], in_=scale_ps[:])
+            else:
+                nc.scalar.copy(out=scale2[:, 1, :], in_=scale_ps[:])
+        turned = psum.tile([P, PACK, P], BF16, name="turned", tag="small", bufs=2)
+        for t in range(PACK):
+            nc.tensor.transpose(turned[:, t, :], rows[:, t::PACK], ident_b[:])
+        spread = psum.tile([P, P], F32, name="spread", tag="small", bufs=2)
+        nc.tensor.transpose(spread[:], top[:].to_broadcast([P, P]), ident[:])
 
         w1_q = keep.tile([P, M], U32, align_bytes=64)
         w1_s = keep.tile([P, M], U8, align_bytes=64)
@@ -126,27 +146,22 @@ def tile_comireclabelawareinterests_kernel(tc, h_bytes, h_scale, w1, tb, g, e, w
         bias = keep.tile([P, PACK, B], F32)
         gain = keep.tile([P, PACK, B], F32)
 
-        def weights():
-            w1_il = keep.tile([P, M, PACK], BF16, align_bytes=64)
-            nc.scalar.copy(out=w1_il[:], in_=w1_raw[:].rearrange("p j n -> p n j"))
-            ws_il = keep.tile([P, D, PACK], BF16, align_bytes=64)
-            nc.vector.tensor_copy(out=ws_il[:], in_=ws_raw[:].rearrange("p j n -> p n j"))
-            nc.vector.quantize_mx(out=w1_q[:].bitcast(FP8X4), scales=w1_s[:], in_=w1_il[:].rearrange("p n j -> p (n j)"))
-            nc.vector.quantize_mx(out=ws_q[:].bitcast(FP8X4), scales=ws_s[:], in_=ws_il[:].rearrange("p n j -> p (n j)"))
+        ws_il = keep.tile([P, D, PACK], BF16, align_bytes=64)
 
-        def token_vectors():
-            top = keep.tile([P, 1], F32)
-            nc.vector.tensor_reduce(out=top[:], in_=rows[:], axis=AXIS.X, op=ALU.max)
-            turned = psum.tile([P, PACK, P], BF16, name="turned", tag="small", bufs=2)
-            for t in range(PACK):
-                nc.tensor.transpose(turned[:, t, :], rows[:, t::PACK], ident_b[:])
-            gain_t = gain[:]
-            nc.vector.tensor_scalar(out=gain_t, in0=turned[:, :, B : 2 * B], scalar1=math.sqrt(S), scalar2=None, op0=ALU.mult)
+        def constants():
+            nc.scalar.copy(out=ws_il[:], in_=ws_raw[:].rearrange("p j n -> p n j"))
+            nc.vector.quantize_mx(out=w1_q[:].bitcast(FP8X4), scales=w1_s[:], in_=w1_il[:].rearrange("p n j -> p (n j)"))
+            nc.vector.tensor_scalar(out=gain[:], in0=turned[:, :, B : 2 * B], scalar1=math.sqrt(S), scalar2=None, op0=ALU.mult)
             tb_t = keep.tile([P, PACK, B], F32)
             nc.vector.tensor_copy(out=tb_t[:], in_=turned[:, :, 0:B])
-            spread = psum.tile([P, P], F32, name="spread", tag="small", bufs=2)
-            nc.tensor.transpose(spread[:], top[:].to_broadcast([P, P]), ident[:])
             nc.vector.scalar_tensor_tensor(out=bias[:], in0=tb_t[:], scalar=-2.0, in1=spread[:, 0:B].unsqueeze(1).to_broadcast([P, PACK, B]), op0=ALU.add, op1=ALU.subtract)
+
+        on_vector = (("EU", 4, 1), ("EU", 4, 2), ("EU", 5, 1), ("EU", 5, 2), ("EU", 6, 1), ("EU", 6, 3), ("O", 6, 0), ("EU", 7, 3), ("O", 7, 1),)
+
+        def eng(name, b, k):
+            return "V" if (name, b, k) in on_vector else "S"
+
+        depth = {"h_il": 3, "e_il": 3, "h_q": 2, "e_q": 3, "a_q": 3, "u_q": 3}
 
         st = [{} for b in range(B)]
 
@@ -176,7 +191,7 @@ def tile_comireclabelawareinterests_kernel(tc, h_bytes, h_scale, w1, tb, g, e, w
         def lay(b, k, key, eng):
             s = st[b]
             if key + "_il" not in s:
-                il = work.tile([P, S * PACK], BF16, name=key + "_il", align_bytes=64)
+                il = work.tile([P, S * PACK], BF16, name=key + "_il", align_bytes=64, bufs=depth[key + "_il"])
                 s[key + "_il"] = il
             o = s[key + "_il"][:].bitcast(F32)[:, 512 * k : 512 * k + 512].rearrange("p (i r u) -> p i r u", i=2, u=2)
             i_ = s[key + str(k)][:].rearrange("p i u r -> p i r u")
@@ -189,8 +204,8 @@ def tile_comireclabelawareinterests_kernel(tc, h_bytes, h_scale, w1, tb, g, e, w
                 nc.vector.tensor_copy(out=o, in_=i_)
 
         def quant(b, key, width):
-            q = work.tile([P, width], U32, name=key + "_q", align_bytes=64)
-            sc = work.tile([P, width], U8, name=key + "_s", align_bytes=64)
+            q = work.tile([P, width], U32, name=key + "_q", align_bytes=64, bufs=depth[key + "_q"])
+            sc = work.tile([P, width], U8, name=key + "_s", align_bytes=64, bufs=depth[key + "_q"])
             nc.vector.quantize_mx(out=q[:].bitcast(FP8X4), scales=sc[:], in_=st[b][key + "_il"][:])
             st[b][key + "_q"] = q
             st[b][key + "_s"] = sc
@@ -334,15 +349,18 @@ def tile_comireclabelawareinterests_kernel(tc, h_bytes, h_scale, w1, tb, g, e, w
         def finish(b, j):
             s = st[b]
             o = work.tile([P, D], F32, name="o", bufs=4)
-            nc.scalar.activation(out=o[:], in_=s["pv" + str(j)][:], func=ACT.Copy, scale=s["al"][:, j : j + 1])
+            if eng("O", b, j) == "S":
+                nc.scalar.activation(out=o[:], in_=s["pv" + str(j)][:], func=ACT.Copy, scale=s["al"][:, j : j + 1])
+            else:
+                nc.vector.tensor_scalar(out=o[:], in0=s["pv" + str(j)][:], scalar1=s["al"][:, j : j + 1], scalar2=None, op0=ALU.mult)
             nc.sync.dma_start(out=out[b, j * P : (j + 1) * P, :], in_=o[:])
 
         steps = {
             "PR": widen,
             "TH": lambda b, k: turn(b, k, st[b]["hv"][:], "h"),
             "TE": lambda b, k: turn(b, k, ebf[b][:], "e"),
-            "EH": lambda b, k: lay(b, k, "h", "S"),
-            "EE": lambda b, k: lay(b, k, "e", "S"),
+            "EH": lambda b, k: lay(b, k, "h", eng("EH", b, k)),
+            "EE": lambda b, k: lay(b, k, "e", eng("EE", b, k)),
             "QH": lambda b, k: quant(b, "h", S),
             "QE": lambda b, k: quant(b, "e", S),
             "K": score,
@@ -356,7 +374,7 @@ def tile_comireclabelawareinterests_kernel(tc, h_bytes, h_scale, w1, tb, g, e, w
             "AT": lambda b, k: weight(b),
             "QA": lambda b, k: quant(b, "a", M),
             "U": project,
-            "EU": lambda b, k: lay_u(b, k, "S"),
+            "EU": lambda b, k: lay_u(b, k, eng("EU", b, k)),
             "QU": lambda b, k: quant(b, "u", D),
             "V": pool_v,
             "QV": logit,
@@ -369,15 +387,15 @@ def tile_comireclabelawareinterests_kernel(tc, h_bytes, h_scale, w1, tb, g, e, w
             "O": finish,
         }
         last = max(lag for name, k, lag in ORDER)
-        ready = set()
+        ready, ready_u = False, False
         for i in range(B + last):
             for name, k, lag in ORDER:
                 b = i - lag
                 if 0 <= b < B:
-                    if name in ("K", "U") and "w" not in ready:
-                        ready.add("w")
-                        weights()
-                    if name == "EX" and "t" not in ready:
-                        ready.add("t")
-                        token_vectors()
+                    if not ready and name in ("QH", "QE", "K", "U"):
+                        ready = True
+                        constants()
+                    if not ready_u and name == "U":
+                        ready_u = True
+                        nc.vector.quantize_mx(out=ws_q[:].bitcast(FP8X4), scales=ws_s[:], in_=ws_il[:].rearrange("p n j -> p (n j)"))
                     steps[name](b, k)

import math
from contextlib import ExitStack

import concourse.mybir as mybir
from concourse.masks import make_identity

B, S, D, M = 8, 512, 512, 256
P = 128
PACK = 4
FLOPS = 2 * B * S * (D * M + D * D + M * D)

F32 = mybir.dt.float32
BF16 = mybir.dt.bfloat16
U32 = mybir.dt.uint32
U8 = mybir.dt.uint8
FP8 = mybir.dt.float8_e4m3fn
FP8X4 = mybir.dt.float8_e4m3fn_x4
ACT = mybir.ActivationFunctionType
ALU = mybir.AluOpType
AXIS = mybir.AxisListType

ORDER = (
    ("EH", 1, 3),
    ("ZR", 0, 5),
    ("EG", 0, 5),
    ("EG", 1, 5),
    ("TA", 0, 4),
    ("EU", 2, 5),
    ("V", 0, 6),
    ("TA", 1, 4),
    ("RC", 0, 5),
    ("U", 1, 5),
    ("EX", 0, 4),
    ("QV", 1, 6),
    ("QV", 0, 6),
    ("U", 0, 5),
    ("EU", 1, 5),
    ("QH", 0, 3),
    ("PR", 1, 1),
    ("U", 3, 5),
    ("TR", 0, 5),
    ("TQ", 0, 6),
    ("EU", 0, 5),
    ("EU", 3, 5),
    ("MN", 0, 6),
    ("TE", 1, 3),
    ("EX", 1, 4),
    ("TH", 0, 2),
    ("XQ", 0, 6),
    ("XE", 0, 6),
    ("AT", 0, 5),
    ("EE", 1, 3),
    ("TE", 0, 3),
    ("RQ", 0, 6),
    ("EH", 0, 2),
    ("TH", 1, 2),
    ("TZ", 0, 4),
    ("QE", 0, 4),
    ("AL", 0, 6),
    ("QA", 0, 5),
    ("K", 0, 3),
    ("QU", 0, 5),
    ("EE", 0, 3),
    ("U", 2, 4),
    ("O", 1, 6),
    ("PR", 0, 0),
    ("O", 0, 6),
    ("V", 1, 5),
    ("K", 1, 3),
)


def tile_comireclabelawareinterests_kernel(tc, h_bytes, h_scale, w1, tb, g, e, ws, c, out):
    nc = tc.nc
    with ExitStack() as ctx:
        keep = ctx.enter_context(tc.tile_pool(name="keep", bufs=1))
        inp = ctx.enter_context(tc.tile_pool(name="inp", bufs=B))
        work = ctx.enter_context(tc.tile_pool(name="work", bufs=3))
        psum = ctx.enter_context(tc.psum_pool(name="psum", bufs=1))
        ctx.enter_context(tc.manual_schedule())

        zero = keep.tile([P, 1], F32)
        nc.vector.memset(zero[:], 0.0)
        scale_rows = keep.tile([P, P], F32)
        nc.vector.memset(scale_rows[:], 0.0)
        rows = keep.tile([P, S], BF16)
        nc.vector.memset(rows[:], 0.0)
        nc.sync.dma_start(out=scale_rows[0 : D // P, :], in_=h_scale.rearrange("a b (k p) -> (a b k) p", p=P))
        nc.sync.dma_start(out=rows[0:B, :], in_=tb)
        nc.sync.dma_start(out=rows[B : 2 * B, :], in_=g)
        warm = keep.tile([P, 1], F32)
        nc.scalar.activation(out=warm[:], in_=zero[:], func=ACT.Exp)
        ident = keep.tile([P, P], F32)
        make_identity(nc, ident[:])
        ident_b = keep.tile([P, P], BF16)
        make_identity(nc, ident_b[:])

        w1_raw = keep.tile([P, PACK, M], BF16)
        ws_raw = keep.tile([P, PACK, D], BF16)
        nc.sync.dma_start(out=w1_raw[:], in_=w1.rearrange("(p j) n -> p j n", j=PACK))
        hbytes, ebf = [], []
        for b in range(B):
            hb = inp.tile([P, PACK * D], U8)
            nc.sync.dma_start(out=hb[:], in_=h_bytes[b].rearrange("(p t) d -> p (t d)", t=PACK))
            hbytes.append(hb)
            eb = inp.tile([P, PACK, D], BF16)
            e_rows = e[b].rearrange("(p t) d -> p t d", t=PACK)
            if b == 0:
                nc.sync.dma_start(out=eb[:, 0:2, :], in_=e_rows[:, 0:2, :])
                nc.sync.dma_start(out=eb[:, 2:4, :], in_=e_rows[:, 2:4, :])
                nc.sync.dma_start(out=ws_raw[:], in_=ws.rearrange("(p j) n -> p j n", j=PACK))
            else:
                nc.sync.dma_start(out=eb[:], in_=e_rows)
            ebf.append(eb)
            if b == 1:
                c_all = keep.tile([P, B, D], BF16)
                nc.sync.dma_start(out=c_all[:].rearrange("p b d -> p (b d)"), in_=c.rearrange("b d -> (b d)").partition_broadcast(P))

        scale_turned = psum.tile([P, P], F32, name="scale_turned", tag="small", bufs=2)
        nc.tensor.transpose(scale_turned[:], scale_rows[:], ident[:])
        scale_col = keep.tile([P, D // P], F32)
        nc.vector.tensor_copy(out=scale_col[:], in_=scale_turned[:, 0 : D // P])
        top = keep.tile([P, 1], F32)
        nc.vector.tensor_reduce(out=top[:], in_=rows[:], axis=AXIS.X, op=ALU.max)
        w1_il = keep.tile([P, M, PACK], BF16, align_bytes=64)
        nc.vector.tensor_copy(out=w1_il[:], in_=w1_raw[:].rearrange("p j n -> p n j"))
        scale2 = keep.tile([P, 2, D], F32)
        for i in range(2):
            scale_ps = psum.tile([P, D], F32, name="scale_ps", tag="bank", bufs=4)
            for k in range(D // P):
                nc.tensor.transpose(scale_ps[:, k * P : (k + 1) * P], scale_col[:, k : k + 1].to_broadcast([P, P]), ident[:])
            if i == 0:
                nc.vector.tensor_copy(out=scale2[:, 0, :], in_=scale_ps[:])
            else:
                nc.scalar.copy(out=scale2[:, 1, :], in_=scale_ps[:])
        turned = psum.tile([P, PACK, P], BF16, name="turned", tag="small", bufs=2)
        for t in range(PACK):
            nc.tensor.transpose(turned[:, t, :], rows[:, t::PACK], ident_b[:])
        spread = psum.tile([P, P], F32, name="spread", tag="small", bufs=2)
        nc.tensor.transpose(spread[:], top[:].to_broadcast([P, P]), ident[:])

        w1_q = keep.tile([P, M], U32, align_bytes=64)
        w1_s = keep.tile([P, M], U8, align_bytes=64)
        ws_q = keep.tile([P, D], U32, align_bytes=64)
        ws_s = keep.tile([P, D], U8, align_bytes=64)
        bias = keep.tile([P, PACK, B], F32)
        gain = keep.tile([P, PACK, B], F32)

        ws_il = keep.tile([P, D, PACK], BF16, align_bytes=64)

        def constants():
            nc.scalar.copy(out=ws_il[:], in_=ws_raw[:].rearrange("p j n -> p n j"))
            nc.vector.quantize_mx(out=w1_q[:].bitcast(FP8X4), scales=w1_s[:], in_=w1_il[:].rearrange("p n j -> p (n j)"))
            nc.vector.tensor_scalar(out=gain[:], in0=turned[:, :, B : 2 * B], scalar1=math.sqrt(S), scalar2=None, op0=ALU.mult)
            tb_t = keep.tile([P, PACK, B], F32)
            nc.vector.tensor_copy(out=tb_t[:], in_=turned[:, :, 0:B])
            nc.vector.scalar_tensor_tensor(out=bias[:], in0=tb_t[:], scalar=-2.0, in1=spread[:, 0:B].unsqueeze(1).to_broadcast([P, PACK, B]), op0=ALU.add, op1=ALU.subtract)

        on_vector = (("EU", 4, 1), ("EU", 4, 2), ("EU", 5, 1), ("EU", 5, 2), ("EU", 6, 1), ("EU", 6, 3), ("O", 6, 0), ("EU", 7, 3), ("O", 7, 1),)

        def eng(name, b, k):
            return "V" if (name, b, k) in on_vector else "S"

        depth = {"h_il": 3, "e_il": 3, "h_q": 2, "e_q": 3, "a_q": 3, "u_q": 3}

        st = [{} for b in range(B)]

        def bank(shape, name):
            return psum.tile(shape, F32, name=name, tag="bank", bufs=4)

        def widen(b, k):
            s = st[b]
            if "hv" not in s:
                hv = work.tile([P, PACK, D], BF16)
                s["hv"] = hv
            nc.vector.tensor_tensor(
                out=s["hv"][:, 2 * k : 2 * k + 2, :].rearrange("p t d -> p (t d)"),
                in0=hbytes[b][:, 2 * k * D : (2 * k + 2) * D].bitcast(FP8),
                in1=scale2[:].rearrange("p t d -> p (t d)"),
                op=ALU.mult,
            )

        def turn(b, k, src, key):
            words = src.rearrange("p t d -> p (t d)").bitcast(F32).rearrange("p (t w) -> p t w", t=PACK)
            pt = bank([P, 2, 2, P], key)
            for i in range(2):
                for u in range(2):
                    nc.tensor.transpose(pt[:, i, u, :], words[:, 2 * k + i, u :: 2], ident[:])
            st[b][key + str(k)] = pt

        def lay(b, k, key, eng):
            s = st[b]
            if key + "_il" not in s:
                il = work.tile([P, S * PACK], BF16, name=key + "_il", align_bytes=64, bufs=depth[key + "_il"])
                s[key + "_il"] = il
            o = s[key + "_il"][:].bitcast(F32)[:, 512 * k : 512 * k + 512].rearrange("p (i r u) -> p i r u", i=2, u=2)
            i_ = s[key + str(k)][:].rearrange("p i u r -> p i r u")
            copy(eng, o, i_)

        def copy(eng, o, i_):
            if eng == "S":
                nc.scalar.copy(out=o, in_=i_)
            else:
                nc.vector.tensor_copy(out=o, in_=i_)

        def quant(b, key, width):
            q = work.tile([P, width], U32, name=key + "_q", align_bytes=64, bufs=depth[key + "_q"])
            sc = work.tile([P, width], U8, name=key + "_s", align_bytes=64, bufs=depth[key + "_q"])
            nc.vector.quantize_mx(out=q[:].bitcast(FP8X4), scales=sc[:], in_=st[b][key + "_il"][:])
            st[b][key + "_q"] = q
            st[b][key + "_s"] = sc

        def mx(o, lq, ls, lc, rq, rs, rc):
            nc.tensor.matmul_mx(out=o, lhsT=lq[:, lc].bitcast(FP8X4), lhsT_scale=ls[:, lc], rhs=rq[:, rc].bitcast(FP8X4), rhs_scale=rs[:, rc], start=True, stop=True)

        def score(b, k):
            pk = bank([P, 2, M], "pk")
            s = st[b]
            for i in range(2):
                t = 2 * k + i
                mx(pk[:, i, :], s["h_q"], s["h_s"], slice(t * P, (t + 1) * P), w1_q, w1_s, slice(0, M))
            s["pk" + str(k)] = pk

        def tanh(b, k):
            s = st[b]
            if "th" not in s:
                th = work.tile([P, PACK, M], F32)
                s["th"] = th
            nc.scalar.activation(out=s["th"][:, 2 * k : 2 * k + 2, :], in_=s["pk" + str(k)][:], func=ACT.Tanh)

        def expo(b, k):
            s = st[b]
            if "ex" not in s:
                ex = work.tile([P, PACK, M], F32)
                s["ex"] = ex
            for t in (2 * k, 2 * k + 1):
                nc.scalar.activation(out=s["ex"][:, t, :], in_=s["th"][:, t, :], func=ACT.Exp, bias=bias[:, t, b : b + 1], scale=2.0)

        def gained(b, k):
            s = st[b]
            if "eg" not in s:
                eg = work.tile([P, PACK, M], F32)
                s["eg"] = eg
            for t in (2 * k, 2 * k + 1):
                nc.vector.tensor_scalar(out=s["eg"][:, t, :], in0=s["ex"][:, t, :], scalar1=gain[:, t, b : b + 1], scalar2=None, op0=ALU.mult)

        def total(b):
            s = st[b]
            pz = psum.tile([P, 512], F32, name="pz", tag="small", bufs=2)
            s["pz"] = pz
            for j in range(2):
                for t in range(PACK):
                    nc.tensor.matmul(pz[:, j * P : (j + 1) * P], lhsT=s["ex"][:, t, j * P : (j + 1) * P], rhs=ident[:], is_transpose=True, start=(t == 0), stop=(t == PACK - 1))

        def sum_z(b):
            s = st[b]
            zz = work.tile([P, 2], F32)
            nc.vector.tensor_reduce(out=zz[:], in_=s["pz"][:, 0:M].rearrange("p (j r) -> p j r", j=2), axis=AXIS.X, op=ALU.add)
            s["zz"] = zz

        def recip(b):
            s = st[b]
            rz = work.tile([P, 2], F32)
            nc.vector.reciprocal(out=rz[:], in_=s["zz"][:])
            s["rz"] = rz

        def spread_total(b):
            s = st[b]
            for j in range(2):
                nc.tensor.transpose(s["pz"][:, M + j * P : M + (j + 1) * P], s["rz"][:, j : j + 1].to_broadcast([P, P]), ident[:])

        def weight(b):
            s = st[b]
            a_il = work.tile([P, M * PACK], BF16, align_bytes=64)
            s["a_il"] = a_il
            nc.vector.tensor_tensor(
                out=a_il[:].rearrange("p (m i t) -> p m t i", i=PACK, t=PACK),
                in0=s["eg"][:].rearrange("p t (m i) -> p m t i", i=PACK),
                in1=s["pz"][:, M : 2 * M].rearrange("p (m i) -> p m i", i=PACK).unsqueeze(2).to_broadcast([P, M // PACK, PACK, PACK]),
                op=ALU.mult,
            )

        def project(b, n):
            s = st[b]
            pu = bank([P, PACK, P], "pu")
            for t in range(PACK):
                mx(pu[:, t, :], s["e_q"], s["e_s"], slice(t * P, (t + 1) * P), ws_q, ws_s, slice(n * P, (n + 1) * P))
            s["pu" + str(n)] = pu

        def lay_u(b, n, eng):
            s = st[b]
            if "u_il" not in s:
                u_il = work.tile([P, D * PACK], BF16, align_bytes=64)
                s["u_il"] = u_il
            copy(eng, s["u_il"][:, 512 * n : 512 * n + 512].rearrange("p (n t) -> p n t", t=PACK), s["pu" + str(n)][:].rearrange("p t n -> p n t"))

        def pool_v(b, j):
            s = st[b]
            pv = psum.tile([P, D], F32, name="pv", tag="pv", bufs=2)
            mx(pv[:], s["a_q"], s["a_s"], slice(j * P, (j + 1) * P), s["u_q"], s["u_s"], slice(0, D))
            s["pv" + str(j)] = pv

        def logit(b, j):
            s = st[b]
            if "nq" not in s:
                nq = work.tile([P, 2], F32)
                s["nq"] = nq
            junk = work.tile([P, D], F32)
            nc.vector.scalar_tensor_tensor(out=junk[:], in0=s["pv" + str(j)][:], scalar=-1.0 / math.sqrt(D), in1=c_all[:, b, :], op0=ALU.mult, op1=ALU.mult, accum_out=s["nq"][:, j : j + 1])

        def spread_logit(b):
            s = st[b]
            pq = psum.tile([P, 512], F32, name="pq", tag="small", bufs=2)
            s["pq"] = pq
            for j in range(2):
                nc.tensor.transpose(pq[:, j * P : (j + 1) * P], s["nq"][:, j : j + 1].to_broadcast([P, P]), ident[:])

        def least(b):
            s = st[b]
            mn = work.tile([P, 1], F32)
            nc.vector.tensor_reduce(out=mn[:], in_=s["pq"][:, 0:M], axis=AXIS.X, op=ALU.min)
            s["mn"] = mn

        def exp_q(b):
            s = st[b]
            xq = work.tile([P, 2], F32)
            nc.scalar.activation(out=xq[:], in_=s["nq"][:], func=ACT.Exp, bias=s["mn"][:], scale=-1.0)
            s["xq"] = xq

        def sum_q(b):
            s = st[b]
            zq = work.tile([P, 1], F32)
            junk_q = work.tile([P, M], F32)
            nc.scalar.activation(out=junk_q[:], in_=s["pq"][:, 0:M], func=ACT.Exp, bias=s["mn"][:], scale=-1.0, accum_out=zq[:])
            s["zq"] = zq

        def recip_q(b):
            s = st[b]
            rq = work.tile([P, 1], F32)
            nc.vector.reciprocal(out=rq[:], in_=s["zq"][:])
            s["rq"] = rq

        def alpha(b):
            s = st[b]
            al = work.tile([P, 2], F32)
            nc.vector.tensor_scalar(out=al[:], in0=s["xq"][:], scalar1=s["rq"][:], scalar2=float(M), op0=ALU.mult, op1=ALU.mult)
            s["al"] = al

        def finish(b, j):
            s = st[b]
            o = work.tile([P, D], F32, name="o", bufs=4)
            if eng("O", b, j) == "S":
                nc.scalar.activation(out=o[:], in_=s["pv" + str(j)][:], func=ACT.Copy, scale=s["al"][:, j : j + 1])
            else:
                nc.vector.tensor_scalar(out=o[:], in0=s["pv" + str(j)][:], scalar1=s["al"][:, j : j + 1], scalar2=None, op0=ALU.mult)
            nc.sync.dma_start(out=out[b, j * P : (j + 1) * P, :], in_=o[:])

        steps = {
            "PR": widen,
            "TH": lambda b, k: turn(b, k, st[b]["hv"][:], "h"),
            "TE": lambda b, k: turn(b, k, ebf[b][:], "e"),
            "EH": lambda b, k: lay(b, k, "h", eng("EH", b, k)),
            "EE": lambda b, k: lay(b, k, "e", eng("EE", b, k)),
            "QH": lambda b, k: quant(b, "h", S),
            "QE": lambda b, k: quant(b, "e", S),
            "K": score,
            "TA": tanh,
            "EX": expo,
            "EG": gained,
            "TZ": lambda b, k: total(b),
            "ZR": lambda b, k: sum_z(b),
            "RC": lambda b, k: recip(b),
            "TR": lambda b, k: spread_total(b),
            "AT": lambda b, k: weight(b),
            "QA": lambda b, k: quant(b, "a", M),
            "U": project,
            "EU": lambda b, k: lay_u(b, k, eng("EU", b, k)),
            "QU": lambda b, k: quant(b, "u", D),
            "V": pool_v,
            "QV": logit,
            "TQ": lambda b, k: spread_logit(b),
            "MN": lambda b, k: least(b),
            "XE": lambda b, k: exp_q(b),
            "XQ": lambda b, k: sum_q(b),
            "RQ": lambda b, k: recip_q(b),
            "AL": lambda b, k: alpha(b),
            "O": finish,
        }
        last = max(lag for name, k, lag in ORDER)
        ready, ready_u = False, False
        for i in range(B + last):
            for name, k, lag in ORDER:
                b = i - lag
                if 0 <= b < B:
                    if not ready and name in ("QH", "QE", "K", "U"):
                        ready = True
                        constants()
                    if not ready_u and name == "U":
                        ready_u = True
                        nc.vector.quantize_mx(out=ws_q[:].bitcast(FP8X4), scales=ws_s[:], in_=ws_il[:].rearrange("p n j -> p (n j)"))
                    steps[name](b, k)
